import numpy as np
import ml_dtypes


def mxq(x, axis, fmt="e4m3"):
    dtype, down = {"e4m3": (ml_dtypes.float8_e4m3fn, 7), "e5m2": (ml_dtypes.float8_e5m2, 14)}[fmt]
    v = np.moveaxis(np.asarray(x, np.float32).astype(ml_dtypes.bfloat16).astype(np.float64), axis, -1)
    blocks = v.reshape(v.shape[:-1] + (-1, 32))
    amax = np.abs(blocks).max(-1, keepdims=True)
    byte = np.maximum(np.where(amax > 0, np.frexp(amax)[1] - 1 + 127, 0) - down, 1)
    scale = np.exp2(byte - 127.0)
    codes = (blocks / scale).astype(np.float32).astype(dtype).astype(np.float64)
    return np.moveaxis((codes * scale).reshape(v.shape), -1, axis)


WIDE = False


def mx_kscale(k):
    if not WIDE:
        return np.ones(k)
    levels = np.array([24, -24, 12, -12, 0])
    if k % 512:
        return np.exp2(np.random.permutation(np.resize(levels, k // 32))).repeat(32)
    a = np.empty((k // 512, 16))
    for p in range(k // 512):
        a[p, :8] = np.random.permutation(np.resize(levels, 8))
        for g in range(8):
            far = levels[np.abs(levels - a[p, g]) >= 10]
            a[p, g + 8] = far[np.random.randint(len(far))]
    return np.exp2(a.ravel()).repeat(32)


def f64(x):
    return np.asarray(x).astype(np.float64)


def striped(idx):
    return np.tile(idx.reshape(-1, 16).T, (8, 1)).astype(np.uint16)


def unstriped(offs):
    return offs[:16].T.reshape(-1).astype(np.int64)


E2M1 = np.array([0.0, 0.5, 1.0, 1.5, 2.0, 3.0, 4.0, 6.0, -0.0, -0.5, -1.0, -1.5, -2.0, -3.0, -4.0, -6.0])


def pack_weight(w, fmt):
    k, n = w.shape
    w = f64(np.asarray(w, np.float32).astype(ml_dtypes.bfloat16)).reshape(k // 32, 32, n)
    amax = np.abs(w).max(1)
    if fmt == "e4m3":
        byte = np.frexp(amax)[1] - 1 + 127 - 7
    else:
        mant, ex = np.frexp(amax / 6.0)
        byte = np.where(mant > 0.5, ex, ex - 1) + 127
    byte = np.clip(np.where(amax > 0, byte, 1), 1, 254)
    scaled = (w * np.exp2(127.0 - byte)[:, None, :]).reshape(k, n).astype(np.float32)
    by_word = np.ascontiguousarray(scaled.reshape(k // 512, 128, 4, n).transpose(0, 1, 3, 2))
    if fmt == "e4m3":
        words = by_word.astype(ml_dtypes.float8_e4m3fn).view(np.uint8)
    else:
        c = by_word.astype(ml_dtypes.float4_e2m1fn).view(np.uint8) & 0xF
        words = (c[..., 0::2] | (c[..., 1::2] << 4)).reshape(k // 512, 128, 2 * n)
    return np.ascontiguousarray(words), np.ascontiguousarray(byte.astype(np.uint8).reshape(k // 512, 16, n))


def unpack_weight(words, scales, fmt):
    g, _, n = scales.shape
    words = np.ascontiguousarray(words).reshape(g, 128, n, -1)
    if fmt == "e4m3":
        vals = words.view(ml_dtypes.float8_e4m3fn).astype(np.float64)
    else:
        nib = np.empty((g, 128, n, 4), np.uint8)
        nib[..., 0::2] = words & 0xF
        nib[..., 1::2] = words >> 4
        vals = E2M1[nib]
    vals = vals * np.repeat(np.exp2(scales.astype(np.float64) - 127.0), 8, axis=1)[..., None]
    return vals.transpose(0, 1, 3, 2).reshape(g * 512, n)


def pack_table4(v):
    words, scales = pack_weight(v, "e2m1")
    g, t = words.shape[0] // 2, v.shape[1]
    return np.ascontiguousarray(words.reshape(g, 2, 128, t, 2).transpose(0, 2, 3, 1, 4).reshape(g, 128, t, 4)), scales


def unpack_table4(words, scales):
    g, _, t, _ = words.shape
    return unpack_weight(words.reshape(g, 128, t, 2, 2).transpose(0, 3, 1, 2, 4).reshape(2 * g, 128, 2 * t), scales, "e2m1")


def planes(y):
    n, m = y.shape
    v = y.astype(np.float32).astype(ml_dtypes.bfloat16).astype(np.float64).reshape(n // 32, 32, m)
    top = np.abs(v).max(1)
    byte = np.clip(np.where(top > 0, np.frexp(top)[1] - 1 + 127 - 7, 1), 1, 254)
    codes = (v * np.exp2(127.0 - byte)[:, None, :]).reshape(n, m).astype(np.float32).astype(ml_dtypes.float8_e4m3fn).view(np.uint8)
    words = codes.reshape(n // 512, 128, 4, m).transpose(0, 1, 3, 2)
    return np.ascontiguousarray(words), np.ascontiguousarray(byte.astype(np.uint8).reshape(n // 512, 16, m))


def silu(f):
    return f / (1.0 + np.exp(-np.maximum(f, -700.0)))


def sigm(f):
    return 1.0 / (1.0 + np.exp(-np.maximum(f, -700.0)))


K, L, N, T, J = 1024, 512, 512, 2048, 1024


def setup_inputs():
    n = np.random.standard_normal
    s = mx_kscale(K)[:, None]
    s2 = mx_kscale(L)[:, None]
    p_tab = pack_table4(n((K, T)) * s)
    p_tab2 = pack_weight(n((L, T)) * s2, "e4m3")
    p_zv = pack_weight(n((K, N)) / np.sqrt(K) / s, "e4m3")
    p_zt = pack_weight(n((L, N)) / np.sqrt(L) / s2, "e2m1")
    p_wv = pack_weight(n((K, N)) / np.sqrt(K) / s, "e2m1")
    return {
        "tab_words": p_tab[0],
        "tab_scales": p_tab[1],
        "tab2_words": p_tab2[0],
        "tab2_scales": p_tab2[1],
        "zv_words": p_zv[0],
        "zv_scales": p_zv[1],
        "zt_words": p_zt[0],
        "zt_scales": p_zt[1],
        "b": (0.3 * n(N)).astype(np.float32),
        "wv_words": p_wv[0],
        "wv_scales": p_wv[1],
        "wt": (n((L, N)) / np.sqrt(L) / s2).astype(np.float32),
        "wgo": np.tile(np.random.uniform(0.5, 2.0, J), (128, 1)).astype(np.float32),
        "offs": striped(np.random.permutation(T)[:J]),
        "offs2": striped(np.random.permutation(T)[:J]),
    }


def reference(tab_words, tab_scales, tab2_words, tab2_scales, zv_words, zv_scales, zt_words, zt_scales, b, wv_words, wv_scales, wt, wgo, offs, offs2):
    idx = unstriped(offs)
    idx2 = unstriped(offs2)
    tab_ = unpack_table4(tab_words, tab_scales)[:, idx]
    tab2_ = unpack_weight(tab2_words, tab2_scales, "e4m3")[:, idx2]
    zv_ = unpack_weight(zv_words, zv_scales, "e4m3")
    zt_ = unpack_weight(zt_words, zt_scales, "e2m1")
    z = zv_.T @ tab_ + zt_.T @ tab2_
    gate = sigm(z + f64(b)[:, None])
    wv_ = unpack_weight(wv_words, wv_scales, "e2m1")
    wt_ = mxq(f64(wt), 0, "e4m3")
    hv = wv_.T @ tab_
    ht = wt_.T @ tab2_
    av = silu(hv)
    at = silu(ht)
    out = np.zeros((N, T))
    out[:, idx] = f64(wgo)[0] * (at + gate * (av - at))
    return (out,) + planes(out)

@@ -1,0 +1,221 @@
+from contextlib import ExitStack
+
+import concourse.mybir as mybir
+
+K, L, N, T, J = 1024, 512, 512, 2048, 1024
+FLOPS = 2 * N * J * (2 * K + 2 * L)
+
+F32 = mybir.dt.float32
+BF16 = mybir.dt.bfloat16
+I32 = mybir.dt.int32
+U32 = mybir.dt.uint32
+U16 = mybir.dt.uint16
+U8 = mybir.dt.uint8
+FP8X4 = mybir.dt.float8_e4m3fn_x4
+FP4X4 = mybir.dt.float4_e2m1fn_x4
+ALU = mybir.AluOpType
+ACT = mybir.ActivationFunctionType
+
+P = 128
+PACK = 4
+HALF = 512
+HALVES = J // HALF
+CHUNK = 512
+QUADRANT = 32
+
+
+def tile_list_gmu_silu_scatP_kernel(
+    tc, tab_words, tab_scales, tab2_words, tab2_scales, zv_words, zv_scales, zt_words, zt_scales,
+    b, wv_words, wv_scales, wt, wgo, offs, offs2, out_0, out_1, out_2,
+):
+    nc = tc.nc
+    with ExitStack() as ctx:
+        lists = ctx.enter_context(tc.tile_pool(name="lists", bufs=1))
+        keep = ctx.enter_context(tc.tile_pool(name="keep", bufs=1))
+        psum = ctx.enter_context(tc.psum_pool(name="psum", bufs=1))
+
+        def held(name, shape, dtype, tag=""):
+            return keep.tile(shape, dtype, name=name, tag=tag or name, align_bytes=64)
+
+        idx = lists.tile([P, J // 16], U16, name="idx")
+        idx2 = lists.tile([P, J // 16], U16, name="idx2")
+
+        tab_sc_win = held("tab_sc_win", [P, T], U8)
+        tab2_sc_win = held("tab2_sc_win", [P, T], U8)
+        tab_sc1 = held("tab_sc1", [P, J], U8)
+        wv_sc_raw = held("wv_sc_raw", [P, 2, N], U8)
+        zv_sc_raw = held("zv_sc_raw", [P, 2, N], U8)
+        zt_sc_raw = held("zt_sc_raw", [P, 1, N], U8)
+        nc.vector.memset(tab_sc_win[:].bitcast(I32), 0)
+        nc.gpsimd.memset(wv_sc_raw[:].bitcast(I32), 0)
+        nc.gpsimd.memset(zt_sc_raw[:].bitcast(I32), 0)
+        nc.vector.memset(tab2_sc_win[:].bitcast(I32), 0)
+        nc.vector.memset(tab_sc1[:].bitcast(I32), 0)
+        nc.vector.memset(zv_sc_raw[:].bitcast(I32), 0)
+        page0 = held("page0", [P, T], F32)
+        nc.vector.memset(page0[:], 0.0)
+
+        def load_scale_rows(queue, tile, scales):
+            for q in range(4):
+                queue.dma_start(
+                    out=tile[QUADRANT * q : QUADRANT * q + 4].bitcast(I32),
+                    in_=scales[:, 4 * q : 4 * q + 4, :].rearrange("a r n -> r a n").bitcast(I32),
+                )
+
+        tab_win = held("tab_win", [P, T], U32, tag="big_b")
+        tab2_win = held("tab2_win", [P, T], U32, tag="big_c")
+        wt_raw = held("wt_raw", [P, PACK, N], F32, tag="big_a")
+        zv_raw = held("zv_raw", [P, 2, N], U32)
+        wv_raw = held("wv_raw", [P, 2, N], U16)
+        zt_raw = held("zt_raw", [P, 1, N], U16)
+        b_raw = held("b_raw", [P, PACK], F32)
+        wgo_sb = held("wgo_sb", [P, J], F32)
+
+        nc.sync.dma_start(idx[:], offs)
+        for q in range(4):
+            nc.scalar.dma_start(
+                out=tab_sc_win[QUADRANT * q : QUADRANT * q + 8, :].bitcast(I32),
+                in_=tab_scales[:, 4 * q : 4 * q + 4, :].bitcast(I32),
+            )
+        nc.sync.dma_start(out=tab_win[:].bitcast(I32), in_=tab_words[0].rearrange("p t i -> p (t i)").bitcast(I32))
+        nc.sync.dma_start(out=wv_raw[:].bitcast(I32), in_=wv_words.rearrange("a p n -> p a n").bitcast(I32))
+        nc.sync.dma_start(out=wt_raw[:], in_=wt.rearrange("(p i) n -> p i n", i=PACK))
+        load_scale_rows(nc.gpsimd, wv_sc_raw, wv_scales)
+        load_scale_rows(nc.gpsimd, zt_sc_raw, zt_scales)
+        for q in range(4):
+            nc.scalar.dma_start(
+                out=tab2_sc_win[QUADRANT * q : QUADRANT * q + 4, :].bitcast(I32),
+                in_=tab2_scales[0, 4 * q : 4 * q + 4, :].bitcast(I32),
+            )
+        nc.sync.dma_start(idx2[:], offs2)
+        nc.sync.dma_start(out=zv_raw[:].bitcast(I32), in_=zv_words.rearrange("a p n i -> p a (n i)").bitcast(I32))
+        nc.sync.dma_start(out=zt_raw[:].bitcast(I32), in_=zt_words.rearrange("a p n -> p a n").bitcast(I32))
+        nc.sync.dma_start(out=b_raw[:], in_=b.rearrange("(p t) -> p t", t=PACK))
+
+        tab_sc = held("tab_sc", [P, J], U8)
+        nc.vector.tensor_copy(out=tab_sc[:], in_=tab_sc_win[:].indirect(idx[:]))
+        for q in range(4):
+            nc.scalar.dma_start(
+                out=tab_sc1[QUADRANT * q : QUADRANT * q + 4, :].bitcast(I32),
+                in_=tab_sc[QUADRANT * q + 4 : QUADRANT * q + 8, :].bitcast(I32),
+            )
+        nc.sync.dma_start(out=tab2_win[:].bitcast(I32), in_=tab2_words[0].rearrange("p t i -> p (t i)").bitcast(I32))
+        load_scale_rows(nc.sync, zv_sc_raw, zv_scales)
+        nc.sync.dma_start(out=wgo_sb[:], in_=wgo)
+        tab_pairs = held("tab_pairs", [P, J], U32)
+        nc.vector.tensor_copy(out=tab_pairs[:], in_=tab_win[:].indirect(idx[:]))
+        tab_cols = held("tab_cols", [P, 2, J], U16)
+        nc.vector.tensor_copy(
+            out=tab_cols[:],
+            in_=tab_pairs[:].bitcast(U16).rearrange("p (j d) -> p d j", d=2),
+        )
+        tab_planes = [tab_sc, tab_sc1]
+
+        def deal(engine_copy, name, raw, passes, dtype):
+            dealt = held(name, [P, passes, PACK, P], dtype)
+            engine_copy(out=dealt[:], in_=raw[:].rearrange("p a (m t) -> p a t m", t=PACK))
+            return dealt
+
+        wv_cols = deal(nc.scalar.copy, "wv_cols", wv_raw, 2, U16)
+        wv_sc = deal(nc.vector.tensor_copy, "wv_sc", wv_sc_raw, 2, U8)
+        wt_bf = held("wt_bf", [P, PACK, P, PACK], BF16)
+        nc.scalar.copy(
+            out=wt_bf[:].rearrange("p t m i -> p m t i"),
+            in_=wt_raw[:].rearrange("p i (m t) -> p m t i", t=PACK),
+        )
+        zv_cols = held("zv_cols", [P, 2, PACK, P], U32)
+        nc.scalar.copy(
+            out=zv_cols[:].rearrange("p a t m -> p a m t"),
+            in_=zv_raw[:].rearrange("p a (m t) -> p a m t", t=PACK),
+        )
+        zt_cols = deal(nc.scalar.copy, "zt_cols", zt_raw, 1, U16)
+        half_b = held("half_b", [P, PACK], F32)
+        nc.gpsimd.tensor_scalar(half_b[:], b_raw[:], 0.5, 0.0, ALU.mult, ALU.add)
+
+        tab2_sc = held("tab2_sc", [P, J], U8)
+        nc.vector.tensor_copy(out=tab2_sc[:], in_=tab2_sc_win[:].indirect(idx2[:]))
+        wt_cols = held("wt_cols", [P, PACK, P], U32)
+        wt_sc = held("wt_sc", [P, PACK, P], U8)
+        nc.vector.quantize_mx(
+            out=wt_cols[:].rearrange("p t m -> p (t m)").bitcast(FP8X4),
+            scales=wt_sc[:].rearrange("p t m -> p (t m)"),
+            in_=wt_bf[:].rearrange("p t m i -> p (t m i)"),
+        )
+        zt_sc = deal(nc.vector.tensor_copy, "zt_sc", zt_sc_raw, 1, U8)
+        zv_sc = deal(nc.vector.tensor_copy, "zv_sc", zv_sc_raw, 2, U8)
+        tab2_cols = []
+        for h in range(HALVES):
+            cols = held(f"tab2_cols{h}", [P, HALF], U32)
+            entries = idx2[:, h * HALF // 16 : (h + 1) * HALF // 16]
+            nc.vector.tensor_copy(out=cols[:], in_=tab2_win[:].indirect(entries))
+            tab2_cols.append(cols)
+
+        pages = [page0]
+        for t, tag in ((1, "big_a"), (2, "big_b"), (3, "big_c")):
+            page = held(f"page{t}", [P, T], F32, tag=tag)
+            nc.gpsimd.memset(page[:], 0.0)
+            pages.append(page)
+
+        av = [held(f"av{t}", [P, J], F32) for t in range(PACK)]
+        at = [held(f"at{t}", [P, J], F32) for t in range(PACK)]
+        th = [held(f"th{t}", [P, J], F32) for t in range(PACK)]
+        units = [(t, h) for t in range(PACK) for h in range(HALVES)]
+
+        for t, h in units:
+            js = slice(h * HALF, (h + 1) * HALF)
+            hv = psum.tile([P, HALF], F32, name="hv", tag="hv", bufs=2)
+            for a in range(2):
+                nc.tensor.matmul_mx(
+                    out=hv[:], lhsT=wv_cols[:, a, t, :].bitcast(FP4X4), lhsT_scale=wv_sc[:, a, t, :],
+                    rhs=tab_cols[:, a, js].bitcast(FP4X4), rhs_scale=tab_planes[a][:, js],
+                    start=(a == 0), stop=(a == 1),
+                )
+            nc.scalar.activation(out=av[t][:, js], in_=hv[:], func=ACT.Silu)
+            ht = psum.tile([P, HALF], F32, name="ht", tag="ht", bufs=2)
+            nc.tensor.matmul_mx(
+                out=ht[:], lhsT=wt_cols[:, t, :].bitcast(FP8X4), lhsT_scale=wt_sc[:, t, :],
+                rhs=tab2_cols[h][:].bitcast(FP8X4), rhs_scale=tab2_sc[:, js], start=True, stop=True,
+            )
+            nc.scalar.activation(out=at[t][:, js], in_=ht[:], func=ACT.Silu)
+            z = psum.tile([P, HALF], F32, name="z", tag="z", bufs=4)
+            for a in range(2):
+                nc.tensor.matmul_mx(
+                    out=z[:], lhsT=zv_cols[:, a, t, :].bitcast(FP8X4), lhsT_scale=zv_sc[:, a, t, :],
+                    rhs=tab_cols[:, a, js].bitcast(FP4X4), rhs_scale=tab_planes[a][:, js],
+                    start=(a == 0), stop=False,
+                )
+            nc.tensor.matmul_mx(
+                out=z[:], lhsT=zt_cols[:, 0, t, :].bitcast(FP4X4), lhsT_scale=zt_sc[:, 0, t, :],
+                rhs=tab2_cols[h][:].bitcast(FP8X4), rhs_scale=tab2_sc[:, js], start=False, stop=True,
+            )
+            nc.scalar.activation(out=th[t][:, js], in_=z[:], func=ACT.Tanh, bias=half_b[:, t : t + 1], scale=0.5)
+
+        rounded = [held(f"rounded{c}", [P, CHUNK, PACK], BF16) for c in range(T // CHUNK)]
+        out_rows = out_0.rearrange("(p t) c -> p t c", t=PACK)
+        for t in range(PACK):
+            halves = [slice(h * HALF, (h + 1) * HALF) for h in range(HALVES)]
+            for js in halves:
+                nc.vector.tensor_tensor(av[t][:, js], av[t][:, js], at[t][:, js], ALU.subtract)
+            for js in halves:
+                nc.vector.scalar_tensor_tensor(th[t][:, js], th[t][:, js], 1.0, av[t][:, js], ALU.add, ALU.mult)
+            for js in halves:
+                nc.vector.scalar_tensor_tensor(av[t][:, js], th[t][:, js], 0.5, at[t][:, js], ALU.mult, ALU.add)
+            nc.vector.tensor_tensor(pages[t][:].indirect(idx[:]), av[t][:], wgo_sb[:], ALU.mult)
+            nc.sync.dma_start(out=out_rows[:, t, :], in_=pages[t][:])
+            for c in range(T // CHUNK):
+                nc.scalar.copy(out=rounded[c][:, :, t], in_=pages[t][:, c * CHUNK : (c + 1) * CHUNK])
+
+        out_sc = held("out_sc", [P, T], U8)
+        out_words = out_1[0].rearrange("p c i -> p (c i)").bitcast(I32)
+        for c in range(T // CHUNK):
+            cs = slice(c * CHUNK, (c + 1) * CHUNK)
+            codes = held(f"codes{c}", [P, CHUNK], U32)
+            nc.vector.quantize_mx(
+                out=codes[:].bitcast(FP8X4), scales=out_sc[:, cs], in_=rounded[c][:].rearrange("p c t -> p (c t)")
+            )
+            nc.sync.dma_start(out=out_words[:, cs], in_=codes[:].bitcast(I32))
+        for q in range(4):
+            nc.scalar.dma_start(
+                out=out_2[0, 4 * q : 4 * q + 4, :].bitcast(I32),
+                in_=out_sc[QUADRANT * q : QUADRANT * q + 4, :].bitcast(I32),
+            )

@@ -20,8 +20,9 @@ P = 128
 PACK = 4
 HALF = 512
 HALVES = J // HALF
-CHUNK = 512
 QUADRANT = 32
+WOVEN = (384, 256)
+DIRECT = (512, 512, 256, 128)
 
 
 def tile_list_gmu_silu_scatP_kernel(
@@ -40,76 +41,82 @@ def tile_list_gmu_silu_scatP_kernel(
         idx = lists.tile([P, J // 16], U16, name="idx")
         idx2 = lists.tile([P, J // 16], U16, name="idx2")
 
-        tab_sc_win = held("tab_sc_win", [P, T], U8)
-        tab2_sc_win = held("tab2_sc_win", [P, T], U8)
-        tab_sc1 = held("tab_sc1", [P, J], U8)
-        wv_sc_raw = held("wv_sc_raw", [P, 2, N], U8)
-        zv_sc_raw = held("zv_sc_raw", [P, 2, N], U8)
-        zt_sc_raw = held("zt_sc_raw", [P, 1, N], U8)
-        nc.vector.memset(tab_sc_win[:].bitcast(I32), 0)
-        nc.gpsimd.memset(wv_sc_raw[:].bitcast(I32), 0)
-        nc.gpsimd.memset(zt_sc_raw[:].bitcast(I32), 0)
-        nc.vector.memset(tab2_sc_win[:].bitcast(I32), 0)
-        nc.vector.memset(tab_sc1[:].bitcast(I32), 0)
-        nc.vector.memset(zv_sc_raw[:].bitcast(I32), 0)
-        page0 = held("page0", [P, T], F32)
-        nc.vector.memset(page0[:], 0.0)
+        tab_sc_win = held("tab_sc_win", [P, T], U8, tag="big_c")
+        tab2_sc_win = held("tab2_sc_win", [P, T], U8, tag="late")
+        tab_sc = held("tab_sc", [P, 2, J], U8)
+        w_sc_raw = held("w_sc_raw", [P, N], U8, tag="big_a")
+        wv_sc = held("wv_sc", [P, 2, PACK, P], U8)
+        zv_sc = held("zv_sc", [P, 2, PACK, P], U8)
+        zt_sc = held("zt_sc", [P, 1, PACK, P], U8)
+        nc.vector.memset(w_sc_raw[64:80, :].bitcast(I32), 0)
+        nc.vector.memset(w_sc_raw[96:128, :].bitcast(I32), 0)
+        nc.gpsimd.memset(tab2_sc_win[:].bitcast(I32), 0)
+        nc.vector.memset(tab_sc_win[32:64, :].bitcast(I32), 0)
+        nc.vector.memset(tab_sc_win[64:128, :].bitcast(I32), 0)
+        nc.vector.memset(wv_sc[:].bitcast(I32), 0)
+        nc.vector.memset(tab_sc[:].bitcast(I32), 0)
+        nc.vector.memset(zv_sc[:].bitcast(I32), 0)
+        nc.vector.memset(zt_sc[:].bitcast(I32), 0)
+        last_page = held("last_page", [P, T], F32)
+        nc.vector.memset(last_page[:], 0.0)
 
-        def load_scale_rows(queue, tile, scales):
-            for q in range(4):
-                queue.dma_start(
-                    out=tile[QUADRANT * q : QUADRANT * q + 4].bitcast(I32),
-                    in_=scales[:, 4 * q : 4 * q + 4, :].rearrange("a r n -> r a n").bitcast(I32),
-                )
-
-        tab_win = held("tab_win", [P, T], U32, tag="big_b")
-        tab2_win = held("tab2_win", [P, T], U32, tag="big_c")
-        wt_raw = held("wt_raw", [P, PACK, N], F32, tag="big_a")
+        tab_win = held("tab_win", [P, T], U32)
         zv_raw = held("zv_raw", [P, 2, N], U32)
         wv_raw = held("wv_raw", [P, 2, N], U16)
         zt_raw = held("zt_raw", [P, 1, N], U16)
         b_raw = held("b_raw", [P, PACK], F32)
-        wgo_sb = held("wgo_sb", [P, J], F32)
 
         nc.sync.dma_start(idx[:], offs)
-        for q in range(4):
-            nc.scalar.dma_start(
-                out=tab_sc_win[QUADRANT * q : QUADRANT * q + 8, :].bitcast(I32),
-                in_=tab_scales[:, 4 * q : 4 * q + 4, :].bitcast(I32),
+        nc.sync.dma_start(out=tab_sc_win[0:32, :].bitcast(I32), in_=tab_scales.rearrange("a q t -> q a t").bitcast(I32))
+        for first, scales in ((0, wv_scales), (32, zv_scales), (80, zt_scales)):
+            rows = 16 * scales.shape[0]
+            nc.sync.dma_start(
+                out=w_sc_raw[first : first + rows, :].bitcast(I32), in_=scales.rearrange("a q n -> q a n").bitcast(I32)
             )
-        nc.sync.dma_start(out=tab_win[:].bitcast(I32), in_=tab_words[0].rearrange("p t i -> p (t i)").bitcast(I32))
-        nc.sync.dma_start(out=wv_raw[:].bitcast(I32), in_=wv_words.rearrange("a p n -> p a n").bitcast(I32))
-        nc.sync.dma_start(out=wt_raw[:], in_=wt.rearrange("(p i) n -> p i n", i=PACK))
-        load_scale_rows(nc.gpsimd, wv_sc_raw, wv_scales)
-        load_scale_rows(nc.gpsimd, zt_sc_raw, zt_scales)
         for q in range(4):
-            nc.scalar.dma_start(
+            nc.gpsimd.dma_start(
                 out=tab2_sc_win[QUADRANT * q : QUADRANT * q + 4, :].bitcast(I32),
                 in_=tab2_scales[0, 4 * q : 4 * q + 4, :].bitcast(I32),
             )
         nc.sync.dma_start(idx2[:], offs2)
-        nc.sync.dma_start(out=zv_raw[:].bitcast(I32), in_=zv_words.rearrange("a p n i -> p a (n i)").bitcast(I32))
-        nc.sync.dma_start(out=zt_raw[:].bitcast(I32), in_=zt_words.rearrange("a p n -> p a n").bitcast(I32))
+        nc.sync.dma_start(out=tab_win[:].bitcast(I32), in_=tab_words[0].rearrange("p t i -> p (t i)").bitcast(I32))
+        nc.sync.dma_start(out=wv_raw[:].bitcast(I32), in_=wv_words.rearrange("a p n -> p a n").bitcast(I32))
         nc.sync.dma_start(out=b_raw[:], in_=b.rearrange("(p t) -> p t", t=PACK))
+        nc.sync.dma_start(out=zt_raw[:].bitcast(I32), in_=zt_words.rearrange("a p n -> p a n").bitcast(I32))
+        nc.sync.dma_start(out=zv_raw[:].bitcast(I32), in_=zv_words.rearrange("a p n i -> p a (n i)").bitcast(I32))
 
-        tab_sc = held("tab_sc", [P, J], U8)
-        nc.vector.tensor_copy(out=tab_sc[:], in_=tab_sc_win[:].indirect(idx[:]))
+        w_sc_rows = held("w_sc_rows", [P, PACK, P], U8)
+        nc.vector.tensor_copy(out=w_sc_rows[:], in_=w_sc_raw[:].rearrange("p (m t) -> p t m", t=PACK))
+
+        def place_weight_scales(queue, plane, first, passes):
+            for q in range(4):
+                row = first + 4 * passes * q
+                queue.dma_start(
+                    out=plane[QUADRANT * q : QUADRANT * q + 4].rearrange("p k t m -> p k (t m)").bitcast(I32),
+                    in_=w_sc_rows[row : row + 4 * passes].rearrange("p t m -> p (t m)").bitcast(I32),
+                )
+
+        place_weight_scales(nc.scalar, wv_sc, 0, 2)
+        place_weight_scales(nc.gpsimd, zt_sc, 80, 1)
+        wt_raw = held("wt_raw", [P, PACK, N], F32, tag="big_a")
+        nc.sync.dma_start(out=wt_raw[:], in_=wt.rearrange("(p i) n -> p i n", i=PACK))
+        place_weight_scales(nc.sync, zv_sc, 32, 2)
+        tab_sc_rows = held("tab_sc_rows", [P, J], U8)
+        nc.vector.tensor_copy(out=tab_sc_rows[:], in_=tab_sc_win[:].indirect(idx[:]))
         for q in range(4):
-            nc.scalar.dma_start(
-                out=tab_sc1[QUADRANT * q : QUADRANT * q + 4, :].bitcast(I32),
-                in_=tab_sc[QUADRANT * q + 4 : QUADRANT * q + 8, :].bitcast(I32),
+            nc.sync.dma_start(
+                out=tab_sc[QUADRANT * q : QUADRANT * q + 4].bitcast(I32),
+                in_=tab_sc_rows[8 * q : 8 * q + 8, :].bitcast(I32),
             )
+        tab2_win = held("tab2_win", [P, T], U32, tag="big_c")
         nc.sync.dma_start(out=tab2_win[:].bitcast(I32), in_=tab2_words[0].rearrange("p t i -> p (t i)").bitcast(I32))
-        load_scale_rows(nc.sync, zv_sc_raw, zv_scales)
-        nc.sync.dma_start(out=wgo_sb[:], in_=wgo)
-        tab_pairs = held("tab_pairs", [P, J], U32)
+        tab_pairs = held("tab_pairs", [P, J], U32, tag="big_b")
         nc.vector.tensor_copy(out=tab_pairs[:], in_=tab_win[:].indirect(idx[:]))
         tab_cols = held("tab_cols", [P, 2, J], U16)
         nc.vector.tensor_copy(
             out=tab_cols[:],
             in_=tab_pairs[:].bitcast(U16).rearrange("p (j d) -> p d j", d=2),
         )
-        tab_planes = [tab_sc, tab_sc1]
 
         def deal(engine_copy, name, raw, passes, dtype):
             dealt = held(name, [P, passes, PACK, P], dtype)
@@ -117,8 +124,7 @@ def tile_list_gmu_silu_scatP_kernel(
             return dealt
 
         wv_cols = deal(nc.scalar.copy, "wv_cols", wv_raw, 2, U16)
-        wv_sc = deal(nc.vector.tensor_copy, "wv_sc", wv_sc_raw, 2, U8)
-        wt_bf = held("wt_bf", [P, PACK, P, PACK], BF16)
+        wt_bf = held("wt_bf", [P, PACK, P, PACK], BF16, tag="big_d")
         nc.scalar.copy(
             out=wt_bf[:].rearrange("p t m i -> p m t i"),
             in_=wt_raw[:].rearrange("p i (m t) -> p m t i", t=PACK),
@@ -134,6 +140,8 @@ def tile_list_gmu_silu_scatP_kernel(
 
         tab2_sc = held("tab2_sc", [P, J], U8)
         nc.vector.tensor_copy(out=tab2_sc[:], in_=tab2_sc_win[:].indirect(idx2[:]))
+        wgo_sb = held("wgo_sb", [P, J], F32, tag="late")
+        nc.sync.dma_start(out=wgo_sb[:], in_=wgo)
         wt_cols = held("wt_cols", [P, PACK, P], U32)
         wt_sc = held("wt_sc", [P, PACK, P], U8)
         nc.vector.quantize_mx(
@@ -141,8 +149,6 @@ def tile_list_gmu_silu_scatP_kernel(
             scales=wt_sc[:].rearrange("p t m -> p (t m)"),
             in_=wt_bf[:].rearrange("p t m i -> p (t m i)"),
         )
-        zt_sc = deal(nc.vector.tensor_copy, "zt_sc", zt_sc_raw, 1, U8)
-        zv_sc = deal(nc.vector.tensor_copy, "zv_sc", zv_sc_raw, 2, U8)
         tab2_cols = []
         for h in range(HALVES):
             cols = held(f"tab2_cols{h}", [P, HALF], U32)
@@ -150,11 +156,12 @@ def tile_list_gmu_silu_scatP_kernel(
             nc.vector.tensor_copy(out=cols[:], in_=tab2_win[:].indirect(entries))
             tab2_cols.append(cols)
 
-        pages = [page0]
-        for t, tag in ((1, "big_a"), (2, "big_b"), (3, "big_c")):
+        pages = []
+        for t, tag in enumerate(("big_b", "big_d", "big_c")):
             page = held(f"page{t}", [P, T], F32, tag=tag)
             nc.gpsimd.memset(page[:], 0.0)
             pages.append(page)
+        pages.append(last_page)
 
         av = [held(f"av{t}", [P, J], F32) for t in range(PACK)]
         at = [held(f"at{t}", [P, J], F32) for t in range(PACK)]
@@ -167,7 +174,7 @@ def tile_list_gmu_silu_scatP_kernel(
             for a in range(2):
                 nc.tensor.matmul_mx(
                     out=hv[:], lhsT=wv_cols[:, a, t, :].bitcast(FP4X4), lhsT_scale=wv_sc[:, a, t, :],
-                    rhs=tab_cols[:, a, js].bitcast(FP4X4), rhs_scale=tab_planes[a][:, js],
+                    rhs=tab_cols[:, a, js].bitcast(FP4X4), rhs_scale=tab_sc[:, a, js],
                     start=(a == 0), stop=(a == 1),
                 )
             nc.scalar.activation(out=av[t][:, js], in_=hv[:], func=ACT.Silu)
@@ -181,7 +188,7 @@ def tile_list_gmu_silu_scatP_kernel(
             for a in range(2):
                 nc.tensor.matmul_mx(
                     out=z[:], lhsT=zv_cols[:, a, t, :].bitcast(FP8X4), lhsT_scale=zv_sc[:, a, t, :],
-                    rhs=tab_cols[:, a, js].bitcast(FP4X4), rhs_scale=tab_planes[a][:, js],
+                    rhs=tab_cols[:, a, js].bitcast(FP4X4), rhs_scale=tab_sc[:, a, js],
                     start=(a == 0), stop=False,
                 )
             nc.tensor.matmul_mx(
@@ -189,27 +196,51 @@ def tile_list_gmu_silu_scatP_kernel(
                 rhs=tab2_cols[h][:].bitcast(FP8X4), rhs_scale=tab2_sc[:, js], start=False, stop=True,
             )
             nc.scalar.activation(out=th[t][:, js], in_=z[:], func=ACT.Tanh, bias=half_b[:, t : t + 1], scale=0.5)
+            if t > 0:
+                nc.scalar.activation(out=th[t][:, js], in_=th[t][:, js], func=ACT.Copy, bias=0.5, scale=0.5)
 
-        rounded = [held(f"rounded{c}", [P, CHUNK, PACK], BF16) for c in range(T // CHUNK)]
+        widths = WOVEN + DIRECT
+        starts = [sum(widths[:c]) for c in range(len(widths))]
+        chunks = [slice(c0, c0 + w) for c0, w in zip(starts, widths)]
+        rounded = [held(f"rounded{c}", [P, w, PACK], BF16) for c, w in enumerate(widths)]
+        flat = [held(f"flat{c}", [P, PACK, w], BF16) for c, w in enumerate(WOVEN)]
         out_rows = out_0.rearrange("(p t) c -> p t c", t=PACK)
         for t in range(PACK):
             halves = [slice(h * HALF, (h + 1) * HALF) for h in range(HALVES)]
+            if t == 0:
+                for js in halves:
+                    nc.vector.tensor_tensor(av[t][:, js], av[t][:, js], at[t][:, js], ALU.subtract)
+                for js in halves:
+                    nc.vector.scalar_tensor_tensor(th[t][:, js], th[t][:, js], 1.0, av[t][:, js], ALU.add, ALU.mult)
+                for js in halves:
+                    nc.vector.scalar_tensor_tensor(av[t][:, js], th[t][:, js], 0.5, at[t][:, js], ALU.mult, ALU.add)
+            else:
+                for js in halves:
+                    nc.gpsimd.tensor_tensor(av[t][:, js], av[t][:, js], at[t][:, js], ALU.subtract)
+                for js in halves:
+                    nc.gpsimd.tensor_tensor(th[t][:, js], th[t][:, js], av[t][:, js], ALU.mult)
+                for js in halves:
+                    nc.gpsimd.tensor_tensor(av[t][:, js], th[t][:, js], at[t][:, js], ALU.add)
             for js in halves:
-                nc.vector.tensor_tensor(av[t][:, js], av[t][:, js], at[t][:, js], ALU.subtract)
-            for js in halves:
-                nc.vector.scalar_tensor_tensor(th[t][:, js], th[t][:, js], 1.0, av[t][:, js], ALU.add, ALU.mult)
-            for js in halves:
-                nc.vector.scalar_tensor_tensor(av[t][:, js], th[t][:, js], 0.5, at[t][:, js], ALU.mult, ALU.add)
-            nc.vector.tensor_tensor(pages[t][:].indirect(idx[:]), av[t][:], wgo_sb[:], ALU.mult)
+                nc.vector.tensor_tensor(th[t][:, js], av[t][:, js], wgo_sb[:, js], ALU.mult)
+            nc.vector.tensor_copy(out=pages[t][:].indirect(idx[:]), in_=th[t][:])
             nc.sync.dma_start(out=out_rows[:, t, :], in_=pages[t][:])
-            for c in range(T // CHUNK):
-                nc.scalar.copy(out=rounded[c][:, :, t], in_=pages[t][:, c * CHUNK : (c + 1) * CHUNK])
+            for c in range(len(WOVEN), len(widths)):
+                nc.scalar.copy(out=rounded[c][:, :, t], in_=pages[t][:, chunks[c]])
+            round_flat = nc.vector.tensor_copy if t == PACK - 1 else nc.scalar.copy
+            for c in range(len(WOVEN)):
+                round_flat(out=flat[c][:, t, :], in_=pages[t][:, chunks[c]])
+        for c in range(len(WOVEN)):
+            nc.vector.tensor_copy(
+                out=rounded[c][:].rearrange("p (c i) t -> p c t i", i=4),
+                in_=flat[c][:].rearrange("p t (c i) -> p c t i", i=4),
+            )
 
         out_sc = held("out_sc", [P, T], U8)
         out_words = out_1[0].rearrange("p c i -> p (c i)").bitcast(I32)
-        for c in range(T // CHUNK):
-            cs = slice(c * CHUNK, (c + 1) * CHUNK)
-            codes = held(f"codes{c}", [P, CHUNK], U32)
+        for c in (0, 2, 1, 3, 4, 5):
+            cs = chunks[c]
+            codes = held(f"codes{c}", [P, widths[c]], U32)
             nc.vector.quantize_mx(
                 out=codes[:].bitcast(FP8X4), scales=out_sc[:, cs], in_=rounded[c][:].rearrange("p c t -> p (c t)")
             )

@@ -21,6 +21,7 @@ PACK = 4
 HALF = 512
 HALVES = J // HALF
 QUADRANT = 32
+SPLIT = 768
 WOVEN = (384, 256)
 DIRECT = (512, 512, 256, 128)
 
@@ -41,75 +42,66 @@ def tile_list_gmu_silu_scatP_kernel(
         idx = lists.tile([P, J // 16], U16, name="idx")
         idx2 = lists.tile([P, J // 16], U16, name="idx2")
 
-        tab_sc_win = held("tab_sc_win", [P, T], U8, tag="big_c")
+        tab_sc_win = held("tab_sc_win", [P, T], U8, tag="big_a")
         tab2_sc_win = held("tab2_sc_win", [P, T], U8, tag="late")
         tab_sc = held("tab_sc", [P, 2, J], U8)
-        w_sc_raw = held("w_sc_raw", [P, N], U8, tag="big_a")
-        wv_sc = held("wv_sc", [P, 2, PACK, P], U8)
-        zv_sc = held("zv_sc", [P, 2, PACK, P], U8)
-        zt_sc = held("zt_sc", [P, 1, PACK, P], U8)
-        nc.vector.memset(w_sc_raw[64:80, :].bitcast(I32), 0)
-        nc.vector.memset(w_sc_raw[96:128, :].bitcast(I32), 0)
+        v_sc_raw = held("v_sc_raw", [P, 2 * N], U8, tag="big_c")
+        v_sc = held("v_sc", [P, 2, 2, PACK, P], U8)
+        zt_sc_raw = held("zt_sc_raw", [P, 1, N], U8)
         nc.gpsimd.memset(tab2_sc_win[:].bitcast(I32), 0)
-        nc.vector.memset(tab_sc_win[32:64, :].bitcast(I32), 0)
-        nc.vector.memset(tab_sc_win[64:128, :].bitcast(I32), 0)
-        nc.vector.memset(wv_sc[:].bitcast(I32), 0)
+        nc.gpsimd.memset(zt_sc_raw[:].bitcast(I32), 0)
+        for rows in (slice(32, 64), slice(64, 128)):
+            nc.vector.memset(v_sc_raw[rows].bitcast(I32), 0)
+            nc.vector.memset(tab_sc_win[rows].bitcast(I32), 0)
+        nc.vector.memset(v_sc[:].bitcast(I32), 0)
         nc.vector.memset(tab_sc[:].bitcast(I32), 0)
-        nc.vector.memset(zv_sc[:].bitcast(I32), 0)
-        nc.vector.memset(zt_sc[:].bitcast(I32), 0)
-        last_page = held("last_page", [P, T], F32)
-        nc.vector.memset(last_page[:], 0.0)
 
-        tab_win = held("tab_win", [P, T], U32)
-        zv_raw = held("zv_raw", [P, 2, N], U32)
+        tab_win = held("tab_win", [P, T], U32, tag="big_e")
+        wt_raw = held("wt_raw", [P, PACK, N], F32)
         wv_raw = held("wv_raw", [P, 2, N], U16)
         zt_raw = held("zt_raw", [P, 1, N], U16)
         b_raw = held("b_raw", [P, PACK], F32)
 
         nc.sync.dma_start(idx[:], offs)
         nc.sync.dma_start(out=tab_sc_win[0:32, :].bitcast(I32), in_=tab_scales.rearrange("a q t -> q a t").bitcast(I32))
-        for first, scales in ((0, wv_scales), (32, zv_scales), (80, zt_scales)):
-            rows = 16 * scales.shape[0]
-            nc.sync.dma_start(
-                out=w_sc_raw[first : first + rows, :].bitcast(I32), in_=scales.rearrange("a q n -> q a n").bitcast(I32)
-            )
-        for q in range(4):
-            nc.gpsimd.dma_start(
-                out=tab2_sc_win[QUADRANT * q : QUADRANT * q + 4, :].bitcast(I32),
-                in_=tab2_scales[0, 4 * q : 4 * q + 4, :].bitcast(I32),
-            )
+        for w, scales in enumerate((wv_scales, zv_scales)):
+            nc.sync.dma_start(out=v_sc_raw[0:32, w * N : (w + 1) * N].bitcast(I32), in_=scales.rearrange("a q n -> q a n").bitcast(I32))
         nc.sync.dma_start(idx2[:], offs2)
-        nc.sync.dma_start(out=tab_win[:].bitcast(I32), in_=tab_words[0].rearrange("p t i -> p (t i)").bitcast(I32))
-        nc.sync.dma_start(out=wv_raw[:].bitcast(I32), in_=wv_words.rearrange("a p n -> p a n").bitcast(I32))
         nc.sync.dma_start(out=b_raw[:], in_=b.rearrange("(p t) -> p t", t=PACK))
+        nc.sync.dma_start(out=tab_win[:].bitcast(I32), in_=tab_words[0].rearrange("p t i -> p (t i)").bitcast(I32))
+        nc.sync.dma_start(out=wt_raw[:], in_=wt.rearrange("(p i) n -> p i n", i=PACK))
+        nc.sync.dma_start(out=wv_raw[:].bitcast(I32), in_=wv_words.rearrange("a p n -> p a n").bitcast(I32))
         nc.sync.dma_start(out=zt_raw[:].bitcast(I32), in_=zt_words.rearrange("a p n -> p a n").bitcast(I32))
-        nc.sync.dma_start(out=zv_raw[:].bitcast(I32), in_=zv_words.rearrange("a p n i -> p a (n i)").bitcast(I32))
-
-        w_sc_rows = held("w_sc_rows", [P, PACK, P], U8)
-        nc.vector.tensor_copy(out=w_sc_rows[:], in_=w_sc_raw[:].rearrange("p (m t) -> p t m", t=PACK))
-
-        def place_weight_scales(queue, plane, first, passes):
+        for plane, scales in ((tab2_sc_win[:], tab2_scales), (zt_sc_raw[:, 0, :], zt_scales)):
             for q in range(4):
-                row = first + 4 * passes * q
-                queue.dma_start(
-                    out=plane[QUADRANT * q : QUADRANT * q + 4].rearrange("p k t m -> p k (t m)").bitcast(I32),
-                    in_=w_sc_rows[row : row + 4 * passes].rearrange("p t m -> p (t m)").bitcast(I32),
+                nc.gpsimd.dma_start(
+                    out=plane[QUADRANT * q : QUADRANT * q + 4, :].bitcast(I32),
+                    in_=scales[0, 4 * q : 4 * q + 4, :].bitcast(I32),
                 )
 
-        place_weight_scales(nc.scalar, wv_sc, 0, 2)
-        place_weight_scales(nc.gpsimd, zt_sc, 80, 1)
-        wt_raw = held("wt_raw", [P, PACK, N], F32, tag="big_a")
-        nc.sync.dma_start(out=wt_raw[:], in_=wt.rearrange("(p i) n -> p i n", i=PACK))
-        place_weight_scales(nc.sync, zv_sc, 32, 2)
-        tab_sc_rows = held("tab_sc_rows", [P, J], U8)
+        def deal(engine_copy, name, raw, passes, dtype, tag=""):
+            dealt = held(name, [P, passes, PACK, P], dtype, tag=tag)
+            engine_copy(out=dealt[:], in_=raw[:].rearrange("p a (m t) -> p a t m", t=PACK))
+            return dealt
+
+        v_sc_rows = held("v_sc_rows", [P, 2, PACK, P], U8)
+        nc.vector.tensor_copy(out=v_sc_rows[:], in_=v_sc_raw[:].rearrange("p (w m t) -> p w t m", w=2, t=PACK))
+        for q in range(4):
+            nc.sync.dma_start(
+                out=v_sc[QUADRANT * q : QUADRANT * q + 4].rearrange("p a w t m -> p a (w t m)").bitcast(I32),
+                in_=v_sc_rows[8 * q : 8 * q + 8].rearrange("p w t m -> p (w t m)").bitcast(I32),
+            )
+        tab2_win = held("tab2_win", [P, T], U32, tag="big_c")
+        nc.sync.dma_start(out=tab2_win[:].bitcast(I32), in_=tab2_words[0].rearrange("p t i -> p (t i)").bitcast(I32))
+        tab_sc_rows = held("tab_sc_rows", [P, J], U8, tag="rows")
         nc.vector.tensor_copy(out=tab_sc_rows[:], in_=tab_sc_win[:].indirect(idx[:]))
+        zv_raw = held("zv_raw", [P, 2, N], U32, tag="big_a")
+        nc.sync.dma_start(out=zv_raw[:].bitcast(I32), in_=zv_words.rearrange("a p n i -> p a (n i)").bitcast(I32))
         for q in range(4):
             nc.sync.dma_start(
                 out=tab_sc[QUADRANT * q : QUADRANT * q + 4].bitcast(I32),
                 in_=tab_sc_rows[8 * q : 8 * q + 8, :].bitcast(I32),
             )
-        tab2_win = held("tab2_win", [P, T], U32, tag="big_c")
-        nc.sync.dma_start(out=tab2_win[:].bitcast(I32), in_=tab2_words[0].rearrange("p t i -> p (t i)").bitcast(I32))
         tab_pairs = held("tab_pairs", [P, J], U32, tag="big_b")
         nc.vector.tensor_copy(out=tab_pairs[:], in_=tab_win[:].indirect(idx[:]))
         tab_cols = held("tab_cols", [P, 2, J], U16)
@@ -118,30 +110,30 @@ def tile_list_gmu_silu_scatP_kernel(
             in_=tab_pairs[:].bitcast(U16).rearrange("p (j d) -> p d j", d=2),
         )
 
-        def deal(engine_copy, name, raw, passes, dtype):
-            dealt = held(name, [P, passes, PACK, P], dtype)
-            engine_copy(out=dealt[:], in_=raw[:].rearrange("p a (m t) -> p a t m", t=PACK))
-            return dealt
-
-        wv_cols = deal(nc.scalar.copy, "wv_cols", wv_raw, 2, U16)
         wt_bf = held("wt_bf", [P, PACK, P, PACK], BF16, tag="big_d")
         nc.scalar.copy(
             out=wt_bf[:].rearrange("p t m i -> p m t i"),
             in_=wt_raw[:].rearrange("p i (m t) -> p m t i", t=PACK),
         )
+        wv_cols = deal(nc.scalar.copy, "wv_cols", wv_raw, 2, U16)
+        zt_cols = deal(nc.scalar.copy, "zt_cols", zt_raw, 1, U16)
         zv_cols = held("zv_cols", [P, 2, PACK, P], U32)
         nc.scalar.copy(
             out=zv_cols[:].rearrange("p a t m -> p a m t"),
             in_=zv_raw[:].rearrange("p a (m t) -> p a m t", t=PACK),
         )
-        zt_cols = deal(nc.scalar.copy, "zt_cols", zt_raw, 1, U16)
         half_b = held("half_b", [P, PACK], F32)
         nc.gpsimd.tensor_scalar(half_b[:], b_raw[:], 0.5, 0.0, ALU.mult, ALU.add)
 
-        tab2_sc = held("tab2_sc", [P, J], U8)
-        nc.vector.tensor_copy(out=tab2_sc[:], in_=tab2_sc_win[:].indirect(idx2[:]))
-        wgo_sb = held("wgo_sb", [P, J], F32, tag="late")
-        nc.sync.dma_start(out=wgo_sb[:], in_=wgo)
+        tab2_sc = held("tab2_sc", [P, J], U8, tag="big_e")
+        tab2_cols = [held(f"tab2_cols{h}", [P, HALF], U32) for h in range(HALVES)]
+
+        def gather_tab2(h):
+            entries = idx2[:, h * HALF // 16 : (h + 1) * HALF // 16]
+            nc.vector.tensor_copy(out=tab2_sc[:, h * HALF : (h + 1) * HALF], in_=tab2_sc_win[:].indirect(entries))
+            nc.vector.tensor_copy(out=tab2_cols[h][:], in_=tab2_win[:].indirect(entries))
+
+        gather_tab2(0)
         wt_cols = held("wt_cols", [P, PACK, P], U32)
         wt_sc = held("wt_sc", [P, PACK, P], U8)
         nc.vector.quantize_mx(
@@ -149,55 +141,54 @@ def tile_list_gmu_silu_scatP_kernel(
             scales=wt_sc[:].rearrange("p t m -> p (t m)"),
             in_=wt_bf[:].rearrange("p t m i -> p (t m i)"),
         )
-        tab2_cols = []
-        for h in range(HALVES):
-            cols = held(f"tab2_cols{h}", [P, HALF], U32)
-            entries = idx2[:, h * HALF // 16 : (h + 1) * HALF // 16]
-            nc.vector.tensor_copy(out=cols[:], in_=tab2_win[:].indirect(entries))
-            tab2_cols.append(cols)
+        gather_tab2(1)
+        wgo_sb = held("wgo_sb", [P, J], F32, tag="late")
+        nc.sync.dma_start(out=wgo_sb[:], in_=wgo)
+
+        zt_sc = deal(nc.vector.tensor_copy, "zt_sc", zt_sc_raw, 1, U8, tag="rows")
 
         pages = []
-        for t, tag in enumerate(("big_b", "big_d", "big_c")):
+        for t, tag in enumerate(("big_b", "big_d", "big_a", "big_c")):
             page = held(f"page{t}", [P, T], F32, tag=tag)
             nc.gpsimd.memset(page[:], 0.0)
             pages.append(page)
-        pages.append(last_page)
 
         av = [held(f"av{t}", [P, J], F32) for t in range(PACK)]
         at = [held(f"at{t}", [P, J], F32) for t in range(PACK)]
         th = [held(f"th{t}", [P, J], F32) for t in range(PACK)]
-        units = [(t, h) for t in range(PACK) for h in range(HALVES)]
+        halves = [slice(h * HALF, (h + 1) * HALF) for h in range(HALVES)]
 
-        for t, h in units:
-            js = slice(h * HALF, (h + 1) * HALF)
-            hv = psum.tile([P, HALF], F32, name="hv", tag="hv", bufs=2)
-            for a in range(2):
+        for t in range(PACK):
+            for h, js in enumerate(halves):
+                hv = psum.tile([P, HALF], F32, name="hv", tag=f"h{t % 2}{h}")
+                for a in range(2):
+                    nc.tensor.matmul_mx(
+                        out=hv[:], lhsT=wv_cols[:, a, t, :].bitcast(FP4X4), lhsT_scale=v_sc[:, a, 0, t, :],
+                        rhs=tab_cols[:, a, js].bitcast(FP4X4), rhs_scale=tab_sc[:, a, js],
+                        start=(a == 0), stop=(a == 1),
+                    )
+                nc.scalar.activation(out=av[t][:, js], in_=hv[:], func=ACT.Silu)
+            for h, js in enumerate(halves):
+                ht = psum.tile([P, HALF], F32, name="ht", tag=f"h{t % 2}{h}")
                 nc.tensor.matmul_mx(
-                    out=hv[:], lhsT=wv_cols[:, a, t, :].bitcast(FP4X4), lhsT_scale=wv_sc[:, a, t, :],
-                    rhs=tab_cols[:, a, js].bitcast(FP4X4), rhs_scale=tab_sc[:, a, js],
-                    start=(a == 0), stop=(a == 1),
+                    out=ht[:], lhsT=wt_cols[:, t, :].bitcast(FP8X4), lhsT_scale=wt_sc[:, t, :],
+                    rhs=tab2_cols[h][:].bitcast(FP8X4), rhs_scale=tab2_sc[:, js], start=True, stop=True,
                 )
-            nc.scalar.activation(out=av[t][:, js], in_=hv[:], func=ACT.Silu)
-            ht = psum.tile([P, HALF], F32, name="ht", tag="ht", bufs=2)
-            nc.tensor.matmul_mx(
-                out=ht[:], lhsT=wt_cols[:, t, :].bitcast(FP8X4), lhsT_scale=wt_sc[:, t, :],
-                rhs=tab2_cols[h][:].bitcast(FP8X4), rhs_scale=tab2_sc[:, js], start=True, stop=True,
-            )
-            nc.scalar.activation(out=at[t][:, js], in_=ht[:], func=ACT.Silu)
-            z = psum.tile([P, HALF], F32, name="z", tag="z", bufs=4)
-            for a in range(2):
+                nc.scalar.activation(out=at[t][:, js], in_=ht[:], func=ACT.Silu)
+                z = psum.tile([P, HALF], F32, name="z", tag="z", bufs=4)
+                for a in range(2):
+                    nc.tensor.matmul_mx(
+                        out=z[:], lhsT=zv_cols[:, a, t, :].bitcast(FP8X4), lhsT_scale=v_sc[:, a, 1, t, :],
+                        rhs=tab_cols[:, a, js].bitcast(FP4X4), rhs_scale=tab_sc[:, a, js],
+                        start=(a == 0), stop=False,
+                    )
                 nc.tensor.matmul_mx(
-                    out=z[:], lhsT=zv_cols[:, a, t, :].bitcast(FP8X4), lhsT_scale=zv_sc[:, a, t, :],
-                    rhs=tab_cols[:, a, js].bitcast(FP4X4), rhs_scale=tab_sc[:, a, js],
-                    start=(a == 0), stop=False,
+                    out=z[:], lhsT=zt_cols[:, 0, t, :].bitcast(FP4X4), lhsT_scale=zt_sc[:, 0, t, :],
+                    rhs=tab2_cols[h][:].bitcast(FP8X4), rhs_scale=tab2_sc[:, js], start=False, stop=True,
                 )
-            nc.tensor.matmul_mx(
-                out=z[:], lhsT=zt_cols[:, 0, t, :].bitcast(FP4X4), lhsT_scale=zt_sc[:, 0, t, :],
-                rhs=tab2_cols[h][:].bitcast(FP8X4), rhs_scale=tab2_sc[:, js], start=False, stop=True,
-            )
-            nc.scalar.activation(out=th[t][:, js], in_=z[:], func=ACT.Tanh, bias=half_b[:, t : t + 1], scale=0.5)
-            if t > 0:
-                nc.scalar.activation(out=th[t][:, js], in_=th[t][:, js], func=ACT.Copy, bias=0.5, scale=0.5)
+                nc.scalar.activation(out=th[t][:, js], in_=z[:], func=ACT.Tanh, bias=half_b[:, t : t + 1], scale=0.5)
+                if t > 0:
+                    nc.scalar.activation(out=th[t][:, js], in_=th[t][:, js], func=ACT.Copy, bias=0.5, scale=0.5)
 
         widths = WOVEN + DIRECT
         starts = [sum(widths[:c]) for c in range(len(widths))]
@@ -206,24 +197,24 @@ def tile_list_gmu_silu_scatP_kernel(
         flat = [held(f"flat{c}", [P, PACK, w], BF16) for c, w in enumerate(WOVEN)]
         out_rows = out_0.rearrange("(p t) c -> p t c", t=PACK)
         for t in range(PACK):
-            halves = [slice(h * HALF, (h + 1) * HALF) for h in range(HALVES)]
+            mix = held(f"mix{t}", [P, J], F32, tag="mix")
             if t == 0:
                 for js in halves:
-                    nc.vector.tensor_tensor(av[t][:, js], av[t][:, js], at[t][:, js], ALU.subtract)
+                    nc.vector.tensor_tensor(mix[:, js], av[t][:, js], at[t][:, js], ALU.subtract)
                 for js in halves:
-                    nc.vector.scalar_tensor_tensor(th[t][:, js], th[t][:, js], 1.0, av[t][:, js], ALU.add, ALU.mult)
+                    nc.vector.scalar_tensor_tensor(mix[:, js], th[t][:, js], 1.0, mix[:, js], ALU.add, ALU.mult)
                 for js in halves:
-                    nc.vector.scalar_tensor_tensor(av[t][:, js], th[t][:, js], 0.5, at[t][:, js], ALU.mult, ALU.add)
+                    nc.vector.scalar_tensor_tensor(mix[:, js], mix[:, js], 0.5, at[t][:, js], ALU.mult, ALU.add)
+                parts = halves
             else:
-                for js in halves:
-                    nc.gpsimd.tensor_tensor(av[t][:, js], av[t][:, js], at[t][:, js], ALU.subtract)
-                for js in halves:
-                    nc.gpsimd.tensor_tensor(th[t][:, js], th[t][:, js], av[t][:, js], ALU.mult)
-                for js in halves:
-                    nc.gpsimd.tensor_tensor(av[t][:, js], th[t][:, js], at[t][:, js], ALU.add)
-            for js in halves:
-                nc.vector.tensor_tensor(th[t][:, js], av[t][:, js], wgo_sb[:, js], ALU.mult)
-            nc.vector.tensor_copy(out=pages[t][:].indirect(idx[:]), in_=th[t][:])
+                parts = [slice(0, SPLIT), slice(SPLIT, J)]
+                nc.gpsimd.tensor_tensor(mix[:], av[t][:], at[t][:], ALU.subtract)
+                nc.gpsimd.tensor_tensor(mix[:], mix[:], th[t][:], ALU.mult)
+                for engine, js in zip((nc.gpsimd, nc.vector), parts):
+                    engine.tensor_tensor(mix[:, js], mix[:, js], at[t][:, js], ALU.add)
+            for js in parts:
+                nc.vector.tensor_tensor(av[t][:, js], mix[:, js], wgo_sb[:, js], ALU.mult)
+            nc.vector.tensor_copy(out=pages[t][:].indirect(idx[:]), in_=av[t][:])
             nc.sync.dma_start(out=out_rows[:, t, :], in_=pages[t][:])
             for c in range(len(WOVEN), len(widths)):
                 nc.scalar.copy(out=rounded[c][:, :, t], in_=pages[t][:, chunks[c]])

@@ -21,7 +21,7 @@ PACK = 4
 HALF = 512
 HALVES = J // HALF
 QUADRANT = 32
-SPLIT = 768
+CLEAR = 512
 WOVEN = (384, 256)
 DIRECT = (512, 512, 256, 128)
 
@@ -150,7 +150,8 @@ def tile_list_gmu_silu_scatP_kernel(
         pages = []
         for t, tag in enumerate(("big_b", "big_d", "big_a", "big_c")):
             page = held(f"page{t}", [P, T], F32, tag=tag)
-            nc.gpsimd.memset(page[:], 0.0)
+            for c0 in range(0, T, CLEAR):
+                nc.gpsimd.memset(page[:, c0 : c0 + CLEAR], 0.0)
             pages.append(page)
 
         av = [held(f"av{t}", [P, J], F32) for t in range(PACK)]
@@ -205,14 +206,12 @@ def tile_list_gmu_silu_scatP_kernel(
                     nc.vector.scalar_tensor_tensor(mix[:, js], th[t][:, js], 1.0, mix[:, js], ALU.add, ALU.mult)
                 for js in halves:
                     nc.vector.scalar_tensor_tensor(mix[:, js], mix[:, js], 0.5, at[t][:, js], ALU.mult, ALU.add)
-                parts = halves
             else:
-                parts = [slice(0, SPLIT), slice(SPLIT, J)]
                 nc.gpsimd.tensor_tensor(mix[:], av[t][:], at[t][:], ALU.subtract)
                 nc.gpsimd.tensor_tensor(mix[:], mix[:], th[t][:], ALU.mult)
-                for engine, js in zip((nc.gpsimd, nc.vector), parts):
-                    engine.tensor_tensor(mix[:, js], mix[:, js], at[t][:, js], ALU.add)
-            for js in parts:
+                for js in halves:
+                    nc.vector.tensor_tensor(mix[:, js], mix[:, js], at[t][:, js], ALU.add)
+            for js in halves:
                 nc.vector.tensor_tensor(av[t][:, js], mix[:, js], wgo_sb[:, js], ALU.mult)
             nc.vector.tensor_copy(out=pages[t][:].indirect(idx[:]), in_=av[t][:])
             nc.sync.dma_start(out=out_rows[:, t, :], in_=pages[t][:])

@@ -1,6 +1,7 @@
 from contextlib import ExitStack
 
 import concourse.mybir as mybir
+from concourse.masks import make_identity
 
 K, L, N, T, J = 1024, 512, 512, 2048, 1024
 FLOPS = 2 * N * J * (2 * K + 2 * L)
@@ -22,8 +23,8 @@ HALF = 512
 HALVES = J // HALF
 QUADRANT = 32
 CLEAR = 512
-WOVEN = (384, 256)
-DIRECT = (512, 512, 256, 128)
+WIDTHS = (512, 512, 384, 256, 256, 128)
+BLOCKS = HALF // P
 
 
 def tile_list_gmu_silu_scatP_kernel(
@@ -43,11 +44,11 @@ def tile_list_gmu_silu_scatP_kernel(
         idx2 = lists.tile([P, J // 16], U16, name="idx2")
 
         tab_sc_win = held("tab_sc_win", [P, T], U8, tag="big_a")
-        tab2_sc_win = held("tab2_sc_win", [P, T], U8, tag="late")
+        tab2_sc_win = held("tab2_sc_win", [P, T], U8)
         tab_sc = held("tab_sc", [P, 2, J], U8)
         v_sc_raw = held("v_sc_raw", [P, 2 * N], U8, tag="big_c")
         v_sc = held("v_sc", [P, 2, 2, PACK, P], U8)
-        zt_sc_raw = held("zt_sc_raw", [P, 1, N], U8)
+        zt_sc_raw = held("zt_sc_raw", [P, 1, N], U8, tag="ident")
         nc.gpsimd.memset(tab2_sc_win[:].bitcast(I32), 0)
         nc.gpsimd.memset(zt_sc_raw[:].bitcast(I32), 0)
         for rows in (slice(32, 64), slice(64, 128)):
@@ -58,7 +59,7 @@ def tile_list_gmu_silu_scatP_kernel(
 
         tab_win = held("tab_win", [P, T], U32, tag="big_e")
         wt_raw = held("wt_raw", [P, PACK, N], F32)
-        wv_raw = held("wv_raw", [P, 2, N], U16)
+        wv_raw = held("wv_raw", [P, 2, N], U16, tag="late")
         zt_raw = held("zt_raw", [P, 1, N], U16)
         b_raw = held("b_raw", [P, PACK], F32)
 
@@ -116,6 +117,8 @@ def tile_list_gmu_silu_scatP_kernel(
             in_=wt_raw[:].rearrange("p i (m t) -> p m t i", t=PACK),
         )
         wv_cols = deal(nc.scalar.copy, "wv_cols", wv_raw, 2, U16)
+        wgo_sb = held("wgo_sb", [P, J], F32, tag="late")
+        nc.sync.dma_start(out=wgo_sb[:], in_=wgo)
         zt_cols = deal(nc.scalar.copy, "zt_cols", zt_raw, 1, U16)
         zv_cols = held("zv_cols", [P, 2, PACK, P], U32)
         nc.scalar.copy(
@@ -142,24 +145,29 @@ def tile_list_gmu_silu_scatP_kernel(
             in_=wt_bf[:].rearrange("p t m i -> p (t m i)"),
         )
         gather_tab2(1)
-        wgo_sb = held("wgo_sb", [P, J], F32, tag="late")
-        nc.sync.dma_start(out=wgo_sb[:], in_=wgo)
 
         zt_sc = deal(nc.vector.tensor_copy, "zt_sc", zt_sc_raw, 1, U8, tag="rows")
 
+        ident = held("ident", [P, P], F32, tag="ident")
+        make_identity(nc, ident[:])
+
         pages = []
-        for t, tag in enumerate(("big_b", "big_d", "big_a", "big_c")):
-            page = held(f"page{t}", [P, T], F32, tag=tag)
+
+        def clear_page(tag):
+            page = held(f"page{len(pages)}", [P, T], F32, tag=tag)
             for c0 in range(0, T, CLEAR):
                 nc.gpsimd.memset(page[:, c0 : c0 + CLEAR], 0.0)
             pages.append(page)
 
+        clear_page("big_b")
+        clear_page("big_d")
+
         av = [held(f"av{t}", [P, J], F32) for t in range(PACK)]
         at = [held(f"at{t}", [P, J], F32) for t in range(PACK)]
-        th = [held(f"th{t}", [P, J], F32) for t in range(PACK)]
+        th = [[held(f"th{t}{h}", [P, HALF], F32) for h in range(HALVES)] for t in range(PACK)]
         halves = [slice(h * HALF, (h + 1) * HALF) for h in range(HALVES)]
 
-        for t in range(PACK):
+        def products(t):
             for h, js in enumerate(halves):
                 hv = psum.tile([P, HALF], F32, name="hv", tag=f"h{t % 2}{h}")
                 for a in range(2):
@@ -176,7 +184,7 @@ def tile_list_gmu_silu_scatP_kernel(
                     rhs=tab2_cols[h][:].bitcast(FP8X4), rhs_scale=tab2_sc[:, js], start=True, stop=True,
                 )
                 nc.scalar.activation(out=at[t][:, js], in_=ht[:], func=ACT.Silu)
-                z = psum.tile([P, HALF], F32, name="z", tag="z", bufs=4)
+                z = psum.tile([P, HALF], F32, name="z", tag="z", bufs=2)
                 for a in range(2):
                     nc.tensor.matmul_mx(
                         out=z[:], lhsT=zv_cols[:, a, t, :].bitcast(FP8X4), lhsT_scale=v_sc[:, a, 1, t, :],
@@ -187,50 +195,104 @@ def tile_list_gmu_silu_scatP_kernel(
                     out=z[:], lhsT=zt_cols[:, 0, t, :].bitcast(FP4X4), lhsT_scale=zt_sc[:, 0, t, :],
                     rhs=tab2_cols[h][:].bitcast(FP8X4), rhs_scale=tab2_sc[:, js], start=False, stop=True,
                 )
-                nc.scalar.activation(out=th[t][:, js], in_=z[:], func=ACT.Tanh, bias=half_b[:, t : t + 1], scale=0.5)
-                if t > 0:
-                    nc.scalar.activation(out=th[t][:, js], in_=th[t][:, js], func=ACT.Copy, bias=0.5, scale=0.5)
+                nc.scalar.activation(out=th[t][h][:], in_=z[:], func=ACT.Tanh, bias=half_b[:, t : t + 1], scale=0.5)
 
-        widths = WOVEN + DIRECT
-        starts = [sum(widths[:c]) for c in range(len(widths))]
-        chunks = [slice(c0, c0 + w) for c0, w in zip(starts, widths)]
-        rounded = [held(f"rounded{c}", [P, w, PACK], BF16) for c, w in enumerate(widths)]
-        flat = [held(f"flat{c}", [P, PACK, w], BF16) for c, w in enumerate(WOVEN)]
         out_rows = out_0.rearrange("(p t) c -> p t c", t=PACK)
-        for t in range(PACK):
-            mix = held(f"mix{t}", [P, J], F32, tag="mix")
-            if t == 0:
-                for js in halves:
-                    nc.vector.tensor_tensor(mix[:, js], av[t][:, js], at[t][:, js], ALU.subtract)
-                for js in halves:
-                    nc.vector.scalar_tensor_tensor(mix[:, js], th[t][:, js], 1.0, mix[:, js], ALU.add, ALU.mult)
-                for js in halves:
-                    nc.vector.scalar_tensor_tensor(mix[:, js], mix[:, js], 0.5, at[t][:, js], ALU.mult, ALU.add)
-            else:
-                nc.gpsimd.tensor_tensor(mix[:], av[t][:], at[t][:], ALU.subtract)
-                nc.gpsimd.tensor_tensor(mix[:], mix[:], th[t][:], ALU.mult)
-                for js in halves:
-                    nc.vector.tensor_tensor(mix[:, js], mix[:, js], at[t][:, js], ALU.add)
-            for js in halves:
-                nc.vector.tensor_tensor(av[t][:, js], mix[:, js], wgo_sb[:, js], ALU.mult)
-            nc.vector.tensor_copy(out=pages[t][:].indirect(idx[:]), in_=av[t][:])
+        entries = [idx[:, h * HALF // 16 : (h + 1) * HALF // 16] for h in range(HALVES)]
+
+        def mix_on_vector(t, h):
+            js = halves[h]
+            mix = held("mix", [P, HALF], F32)
+            nc.vector.tensor_tensor(mix[:], av[t][:, js], at[t][:, js], ALU.subtract)
+            nc.vector.scalar_tensor_tensor(mix[:], th[t][h][:], 1.0, mix[:], ALU.add, ALU.mult)
+            nc.vector.scalar_tensor_tensor(mix[:], mix[:], 0.5, at[t][:, js], ALU.mult, ALU.add)
+            nc.vector.tensor_tensor(av[t][:, js], mix[:], wgo_sb[:, js], ALU.mult)
+
+        def scatter(t, h):
+            nc.vector.tensor_copy(out=pages[t][:].indirect(entries[h]), in_=av[t][:, halves[h]])
+
+        def store_page(t):
             nc.sync.dma_start(out=out_rows[:, t, :], in_=pages[t][:])
-            for c in range(len(WOVEN), len(widths)):
-                nc.scalar.copy(out=rounded[c][:, :, t], in_=pages[t][:, chunks[c]])
-            round_flat = nc.vector.tensor_copy if t == PACK - 1 else nc.scalar.copy
-            for c in range(len(WOVEN)):
-                round_flat(out=flat[c][:, t, :], in_=pages[t][:, chunks[c]])
-        for c in range(len(WOVEN)):
-            nc.vector.tensor_copy(
+
+        wgo_col = held("wgo_col", [P, HALVES, BLOCKS], F32)
+
+        def turn_wgo():
+            for h in range(HALVES):
+                bank = psum.tile([P, BLOCKS, P], F32, name="wgo_turned", tag=("turned", "back")[h])
+                for k in range(BLOCKS):
+                    j0 = h * HALF + k * P
+                    nc.tensor.transpose(bank[:, k, :], wgo_sb[:, j0 : j0 + P], ident[:])
+                nc.scalar.activation(out=wgo_col[:, h, :], in_=bank[:, :, 0], func=ACT.Copy, scale=0.5)
+
+        def mix_beside_vector(t, h, tag):
+            js = halves[h]
+            mix = held(f"mix{t}{h}", [P, HALF], F32, tag=tag)
+            nc.gpsimd.tensor_tensor(mix[:], av[t][:, js], at[t][:, js], ALU.subtract)
+            nc.gpsimd.tensor_tensor(mix[:], mix[:], th[t][h][:], ALU.mult)
+            turned = psum.tile([P, BLOCKS, P], F32, name="turned", tag="turned")
+            for k in range(BLOCKS):
+                ks = slice(h * HALF + k * P, h * HALF + (k + 1) * P)
+                nc.tensor.matmul(turned[:, k, :], av[t][:, ks], ident[:], start=True, stop=False, is_transpose=True)
+                nc.tensor.matmul(turned[:, k, :], at[t][:, ks], ident[:], start=False, stop=False, is_transpose=True)
+                nc.tensor.matmul(turned[:, k, :], mix[:, k * P : (k + 1) * P], ident[:], start=False, stop=True, is_transpose=True)
+            weighted = held(f"weighted{t}{h}", [P, BLOCKS, P], F32, tag="flat" if (t, h) == (2, 1) else f"weighted{h}")
+            for k in range(BLOCKS):
+                nc.scalar.activation(out=weighted[:, k, :], in_=turned[:, k, :], func=ACT.Copy, scale=wgo_col[:, h, k : k + 1])
+            back = psum.tile([P, BLOCKS, P], F32, name="back", tag="back")
+            for k in range(BLOCKS):
+                nc.tensor.transpose(back[:, k, :], weighted[:, k, :], ident[:])
+            nc.scalar.copy(out=av[t][:, js], in_=back[:].rearrange("p k m -> p (k m)"))
+
+        products(0)
+        mix_on_vector(0, 1)
+        scatter(0, 1)
+        products(1)
+        turn_wgo()
+        mix_beside_vector(0, 0, "mix00")
+        scatter(0, 0)
+        store_page(0)
+        products(2)
+        clear_page("th00")
+        mix_beside_vector(1, 0, "mix")
+        scatter(1, 0)
+        mix_beside_vector(1, 1, "th10")
+        scatter(1, 1)
+        store_page(1)
+        products(3)
+        mix_beside_vector(2, 0, "th11")
+        scatter(2, 0)
+        mix_beside_vector(2, 1, "th20")
+        scatter(2, 1)
+        store_page(2)
+        mix_beside_vector(3, 0, "th21")
+        mix_beside_vector(3, 1, "th30")
+        clear_page("at2")
+        scatter(3, 0)
+        scatter(3, 1)
+        store_page(3)
+
+        starts = [sum(WIDTHS[:c]) for c in range(len(WIDTHS))]
+        chunks = [slice(c0, c0 + w) for c0, w in zip(starts, WIDTHS)]
+        flat = held("flat", [P, PACK * T], BF16, tag="flat")
+        planes = [flat[:, PACK * cs.start : PACK * cs.stop].rearrange("p (t c) -> p t c", t=PACK) for cs in chunks]
+        for t in range(PACK - 1):
+            for c, cs in enumerate(chunks):
+                nc.scalar.copy(out=planes[c][:, t, :], in_=pages[t][:, cs])
+        copies = [nc.vector.tensor_copy if c % 2 == 0 else nc.scalar.copy for c in range(len(WIDTHS))]
+        for c, cs in enumerate(chunks):
+            copies[c](out=planes[c][:, PACK - 1, :], in_=pages[PACK - 1][:, cs])
+        rounded = [held(f"rounded{c}", [P, w, PACK], BF16) for c, w in enumerate(WIDTHS)]
+        for c in range(len(WIDTHS)):
+            copies[c](
                 out=rounded[c][:].rearrange("p (c i) t -> p c t i", i=4),
-                in_=flat[c][:].rearrange("p t (c i) -> p c t i", i=4),
+                in_=planes[c].rearrange("p t (c i) -> p c t i", i=4),
             )
 
         out_sc = held("out_sc", [P, T], U8)
         out_words = out_1[0].rearrange("p c i -> p (c i)").bitcast(I32)
-        for c in (0, 2, 1, 3, 4, 5):
+        for c in range(len(WIDTHS)):
             cs = chunks[c]
-            codes = held(f"codes{c}", [P, widths[c]], U32)
+            codes = held(f"codes{c}", [P, WIDTHS[c]], U32)
             nc.vector.quantize_mx(
                 out=codes[:].bitcast(FP8X4), scales=out_sc[:, cs], in_=rounded[c][:].rearrange("p c t -> p (c t)")
             )

from contextlib import ExitStack

import concourse.mybir as mybir
from concourse.masks import make_identity

K, L, N, T, J = 1024, 512, 512, 2048, 1024
FLOPS = 2 * N * J * (2 * K + 2 * L)

F32 = mybir.dt.float32
BF16 = mybir.dt.bfloat16
I32 = mybir.dt.int32
U32 = mybir.dt.uint32
U16 = mybir.dt.uint16
U8 = mybir.dt.uint8
FP8X4 = mybir.dt.float8_e4m3fn_x4
FP4X4 = mybir.dt.float4_e2m1fn_x4
ALU = mybir.AluOpType
ACT = mybir.ActivationFunctionType

P = 128
PACK = 4
HALF = 512
HALVES = J // HALF
QUADRANT = 32
CLEAR = 512
WIDTHS = (512, 512, 384, 256, 256, 128)
BLOCKS = HALF // P


def tile_list_gmu_silu_scatP_kernel(
    tc, tab_words, tab_scales, tab2_words, tab2_scales, zv_words, zv_scales, zt_words, zt_scales,
    b, wv_words, wv_scales, wt, wgo, offs, offs2, out_0, out_1, out_2,
):
    nc = tc.nc
    with ExitStack() as ctx:
        lists = ctx.enter_context(tc.tile_pool(name="lists", bufs=1))
        keep = ctx.enter_context(tc.tile_pool(name="keep", bufs=1))
        psum = ctx.enter_context(tc.psum_pool(name="psum", bufs=1))

        def held(name, shape, dtype, tag=""):
            return keep.tile(shape, dtype, name=name, tag=tag or name, align_bytes=64)

        idx = lists.tile([P, J // 16], U16, name="idx")
        idx2 = lists.tile([P, J // 16], U16, name="idx2")

        tab_sc_win = held("tab_sc_win", [P, T], U8, tag="big_a")
        tab2_sc_win = held("tab2_sc_win", [P, T], U8)
        tab_sc = held("tab_sc", [P, 2, J], U8)
        v_sc_raw = held("v_sc_raw", [P, 2 * N], U8, tag="big_c")
        v_sc = held("v_sc", [P, 2, 2, PACK, P], U8)
        zt_sc_raw = held("zt_sc_raw", [P, 1, N], U8, tag="ident")
        nc.gpsimd.memset(tab2_sc_win[:].bitcast(I32), 0)
        nc.gpsimd.memset(zt_sc_raw[:].bitcast(I32), 0)
        for rows in (slice(32, 64), slice(64, 128)):
            nc.vector.memset(v_sc_raw[rows].bitcast(I32), 0)
            nc.vector.memset(tab_sc_win[rows].bitcast(I32), 0)
        nc.vector.memset(v_sc[:].bitcast(I32), 0)
        nc.vector.memset(tab_sc[:].bitcast(I32), 0)

        tab_win = held("tab_win", [P, T], U32, tag="big_e")
        wt_raw = held("wt_raw", [P, PACK, N], F32)
        wv_raw = held("wv_raw", [P, 2, N], U16, tag="late")
        zt_raw = held("zt_raw", [P, 1, N], U16)
        b_raw = held("b_raw", [P, PACK], F32)

        nc.sync.dma_start(idx[:], offs)
        nc.sync.dma_start(out=tab_sc_win[0:32, :].bitcast(I32), in_=tab_scales.rearrange("a q t -> q a t").bitcast(I32))
        for w, scales in enumerate((wv_scales, zv_scales)):
            nc.sync.dma_start(out=v_sc_raw[0:32, w * N : (w + 1) * N].bitcast(I32), in_=scales.rearrange("a q n -> q a n").bitcast(I32))
        nc.sync.dma_start(idx2[:], offs2)
        nc.sync.dma_start(out=b_raw[:], in_=b.rearrange("(p t) -> p t", t=PACK))
        nc.sync.dma_start(out=tab_win[:].bitcast(I32), in_=tab_words[0].rearrange("p t i -> p (t i)").bitcast(I32))
        nc.sync.dma_start(out=wt_raw[:], in_=wt.rearrange("(p i) n -> p i n", i=PACK))
        nc.sync.dma_start(out=wv_raw[:].bitcast(I32), in_=wv_words.rearrange("a p n -> p a n").bitcast(I32))
        nc.sync.dma_start(out=zt_raw[:].bitcast(I32), in_=zt_words.rearrange("a p n -> p a n").bitcast(I32))
        for plane, scales in ((tab2_sc_win[:], tab2_scales), (zt_sc_raw[:, 0, :], zt_scales)):
            for q in range(4):
                nc.gpsimd.dma_start(
                    out=plane[QUADRANT * q : QUADRANT * q + 4, :].bitcast(I32),
                    in_=scales[0, 4 * q : 4 * q + 4, :].bitcast(I32),
                )

        def deal(engine_copy, name, raw, passes, dtype, tag=""):
            dealt = held(name, [P, passes, PACK, P], dtype, tag=tag)
            engine_copy(out=dealt[:], in_=raw[:].rearrange("p a (m t) -> p a t m", t=PACK))
            return dealt

        v_sc_rows = held("v_sc_rows", [P, 2, PACK, P], U8)
        nc.vector.tensor_copy(out=v_sc_rows[:], in_=v_sc_raw[:].rearrange("p (w m t) -> p w t m", w=2, t=PACK))
        for q in range(4):
            nc.sync.dma_start(
                out=v_sc[QUADRANT * q : QUADRANT * q + 4].rearrange("p a w t m -> p a (w t m)").bitcast(I32),
                in_=v_sc_rows[8 * q : 8 * q + 8].rearrange("p w t m -> p (w t m)").bitcast(I32),
            )
        tab2_win = held("tab2_win", [P, T], U32, tag="big_c")
        nc.sync.dma_start(out=tab2_win[:].bitcast(I32), in_=tab2_words[0].rearrange("p t i -> p (t i)").bitcast(I32))
        tab_sc_rows = held("tab_sc_rows", [P, J], U8, tag="rows")
        nc.vector.tensor_copy(out=tab_sc_rows[:], in_=tab_sc_win[:].indirect(idx[:]))
        zv_raw = held("zv_raw", [P, 2, N], U32, tag="big_a")
        nc.sync.dma_start(out=zv_raw[:].bitcast(I32), in_=zv_words.rearrange("a p n i -> p a (n i)").bitcast(I32))
        for q in range(4):
            nc.sync.dma_start(
                out=tab_sc[QUADRANT * q : QUADRANT * q + 4].bitcast(I32),
                in_=tab_sc_rows[8 * q : 8 * q + 8, :].bitcast(I32),
            )
        tab_pairs = held("tab_pairs", [P, J], U32, tag="big_b")
        nc.vector.tensor_copy(out=tab_pairs[:], in_=tab_win[:].indirect(idx[:]))
        tab_cols = held("tab_cols", [P, 2, J], U16)
        nc.vector.tensor_copy(
            out=tab_cols[:],
            in_=tab_pairs[:].bitcast(U16).rearrange("p (j d) -> p d j", d=2),
        )

        wt_bf = held("wt_bf", [P, PACK, P, PACK], BF16, tag="big_d")
        nc.scalar.copy(
            out=wt_bf[:].rearrange("p t m i -> p m t i"),
            in_=wt_raw[:].rearrange("p i (m t) -> p m t i", t=PACK),
        )
        wv_cols = deal(nc.scalar.copy, "wv_cols", wv_raw, 2, U16)
        wgo_sb = held("wgo_sb", [P, J], F32, tag="late")
        nc.sync.dma_start(out=wgo_sb[:], in_=wgo)
        zt_cols = deal(nc.scalar.copy, "zt_cols", zt_raw, 1, U16)
        zv_cols = held("zv_cols", [P, 2, PACK, P], U32)
        nc.scalar.copy(
            out=zv_cols[:].rearrange("p a t m -> p a m t"),
            in_=zv_raw[:].rearrange("p a (m t) -> p a m t", t=PACK),
        )
        half_b = held("half_b", [P, PACK], F32)
        nc.gpsimd.tensor_scalar(half_b[:], b_raw[:], 0.5, 0.0, ALU.mult, ALU.add)

        tab2_sc = held("tab2_sc", [P, J], U8, tag="big_e")
        tab2_cols = [held(f"tab2_cols{h}", [P, HALF], U32) for h in range(HALVES)]

        def gather_tab2(h):
            entries = idx2[:, h * HALF // 16 : (h + 1) * HALF // 16]
            nc.vector.tensor_copy(out=tab2_sc[:, h * HALF : (h + 1) * HALF], in_=tab2_sc_win[:].indirect(entries))
            nc.vector.tensor_copy(out=tab2_cols[h][:], in_=tab2_win[:].indirect(entries))

        gather_tab2(0)
        wt_cols = held("wt_cols", [P, PACK, P], U32)
        wt_sc = held("wt_sc", [P, PACK, P], U8)
        nc.vector.quantize_mx(
            out=wt_cols[:].rearrange("p t m -> p (t m)").bitcast(FP8X4),
            scales=wt_sc[:].rearrange("p t m -> p (t m)"),
            in_=wt_bf[:].rearrange("p t m i -> p (t m i)"),
        )
        gather_tab2(1)

        zt_sc = deal(nc.vector.tensor_copy, "zt_sc", zt_sc_raw, 1, U8, tag="rows")

        ident = held("ident", [P, P], F32, tag="ident")
        make_identity(nc, ident[:])

        pages = []

        def clear_page(tag):
            page = held(f"page{len(pages)}", [P, T], F32, tag=tag)
            for c0 in range(0, T, CLEAR):
                nc.gpsimd.memset(page[:, c0 : c0 + CLEAR], 0.0)
            pages.append(page)

        clear_page("big_b")
        clear_page("big_d")

        av = [held(f"av{t}", [P, J], F32) for t in range(PACK)]
        at = [held(f"at{t}", [P, J], F32) for t in range(PACK)]
        th = [[held(f"th{t}{h}", [P, HALF], F32) for h in range(HALVES)] for t in range(PACK)]
        halves = [slice(h * HALF, (h + 1) * HALF) for h in range(HALVES)]

        def products(t):
            for h, js in enumerate(halves):
                hv = psum.tile([P, HALF], F32, name="hv", tag=f"h{t % 2}{h}")
                for a in range(2):
                    nc.tensor.matmul_mx(
                        out=hv[:], lhsT=wv_cols[:, a, t, :].bitcast(FP4X4), lhsT_scale=v_sc[:, a, 0, t, :],
                        rhs=tab_cols[:, a, js].bitcast(FP4X4), rhs_scale=tab_sc[:, a, js],
                        start=(a == 0), stop=(a == 1),
                    )
                nc.scalar.activation(out=av[t][:, js], in_=hv[:], func=ACT.Silu)
            for h, js in enumerate(halves):
                ht = psum.tile([P, HALF], F32, name="ht", tag=f"h{t % 2}{h}")
                nc.tensor.matmul_mx(
                    out=ht[:], lhsT=wt_cols[:, t, :].bitcast(FP8X4), lhsT_scale=wt_sc[:, t, :],
                    rhs=tab2_cols[h][:].bitcast(FP8X4), rhs_scale=tab2_sc[:, js], start=True, stop=True,
                )
                nc.scalar.activation(out=at[t][:, js], in_=ht[:], func=ACT.Silu)
                z = psum.tile([P, HALF], F32, name="z", tag="z", bufs=2)
                for a in range(2):
                    nc.tensor.matmul_mx(
                        out=z[:], lhsT=zv_cols[:, a, t, :].bitcast(FP8X4), lhsT_scale=v_sc[:, a, 1, t, :],
                        rhs=tab_cols[:, a, js].bitcast(FP4X4), rhs_scale=tab_sc[:, a, js],
                        start=(a == 0), stop=False,
                    )
                nc.tensor.matmul_mx(
                    out=z[:], lhsT=zt_cols[:, 0, t, :].bitcast(FP4X4), lhsT_scale=zt_sc[:, 0, t, :],
                    rhs=tab2_cols[h][:].bitcast(FP8X4), rhs_scale=tab2_sc[:, js], start=False, stop=True,
                )
                nc.scalar.activation(out=th[t][h][:], in_=z[:], func=ACT.Tanh, bias=half_b[:, t : t + 1], scale=0.5)

        out_rows = out_0.rearrange("(p t) c -> p t c", t=PACK)
        entries = [idx[:, h * HALF // 16 : (h + 1) * HALF // 16] for h in range(HALVES)]

        def mix_on_vector(t, h):
            js = halves[h]
            mix = held("mix", [P, HALF], F32)
            nc.vector.tensor_tensor(mix[:], av[t][:, js], at[t][:, js], ALU.subtract)
            nc.vector.scalar_tensor_tensor(mix[:], th[t][h][:], 1.0, mix[:], ALU.add, ALU.mult)
            nc.vector.scalar_tensor_tensor(mix[:], mix[:], 0.5, at[t][:, js], ALU.mult, ALU.add)
            nc.vector.tensor_tensor(av[t][:, js], mix[:], wgo_sb[:, js], ALU.mult)

        def scatter(t, h):
            nc.vector.tensor_copy(out=pages[t][:].indirect(entries[h]), in_=av[t][:, halves[h]])

        def store_page(t):
            nc.sync.dma_start(out=out_rows[:, t, :], in_=pages[t][:])

        wgo_col = held("wgo_col", [P, HALVES, BLOCKS], F32)

        def turn_wgo():
            for h in range(HALVES):
                bank = psum.tile([P, BLOCKS, P], F32, name="wgo_turned", tag=("turned", "back")[h])
                for k in range(BLOCKS):
                    j0 = h * HALF + k * P
                    nc.tensor.transpose(bank[:, k, :], wgo_sb[:, j0 : j0 + P], ident[:])
                nc.scalar.activation(out=wgo_col[:, h, :], in_=bank[:, :, 0], func=ACT.Copy, scale=0.5)

        def mix_beside_vector(t, h, tag):
            js = halves[h]
            mix = held(f"mix{t}{h}", [P, HALF], F32, tag=tag)
            nc.gpsimd.tensor_tensor(mix[:], av[t][:, js], at[t][:, js], ALU.subtract)
            nc.gpsimd.tensor_tensor(mix[:], mix[:], th[t][h][:], ALU.mult)
            turned = psum.tile([P, BLOCKS, P], F32, name="turned", tag="turned")
            for k in range(BLOCKS):
                ks = slice(h * HALF + k * P, h * HALF + (k + 1) * P)
                nc.tensor.matmul(turned[:, k, :], av[t][:, ks], ident[:], start=True, stop=False, is_transpose=True)
                nc.tensor.matmul(turned[:, k, :], at[t][:, ks], ident[:], start=False, stop=False, is_transpose=True)
                nc.tensor.matmul(turned[:, k, :], mix[:, k * P : (k + 1) * P], ident[:], start=False, stop=True, is_transpose=True)
            weighted = held(f"weighted{t}{h}", [P, BLOCKS, P], F32, tag="flat" if (t, h) == (2, 1) else f"weighted{h}")
            for k in range(BLOCKS):
                nc.scalar.activation(out=weighted[:, k, :], in_=turned[:, k, :], func=ACT.Copy, scale=wgo_col[:, h, k : k + 1])
            back = psum.tile([P, BLOCKS, P], F32, name="back", tag="back")
            for k in range(BLOCKS):
                nc.tensor.transpose(back[:, k, :], weighted[:, k, :], ident[:])
            nc.scalar.copy(out=av[t][:, js], in_=back[:].rearrange("p k m -> p (k m)"))

        products(0)
        mix_on_vector(0, 1)
        scatter(0, 1)
        products(1)
        turn_wgo()
        mix_beside_vector(0, 0, "mix00")
        scatter(0, 0)
        store_page(0)
        products(2)
        clear_page("th00")
        mix_beside_vector(1, 0, "mix")
        scatter(1, 0)
        mix_beside_vector(1, 1, "th10")
        scatter(1, 1)
        store_page(1)
        products(3)
        mix_beside_vector(2, 0, "th11")
        scatter(2, 0)
        mix_beside_vector(2, 1, "th20")
        scatter(2, 1)
        store_page(2)
        mix_beside_vector(3, 0, "th21")
        mix_beside_vector(3, 1, "th30")
        clear_page("at2")
        scatter(3, 0)
        scatter(3, 1)
        store_page(3)

        starts = [sum(WIDTHS[:c]) for c in range(len(WIDTHS))]
        chunks = [slice(c0, c0 + w) for c0, w in zip(starts, WIDTHS)]
        flat = held("flat", [P, PACK * T], BF16, tag="flat")
        planes = [flat[:, PACK * cs.start : PACK * cs.stop].rearrange("p (t c) -> p t c", t=PACK) for cs in chunks]
        for t in range(PACK - 1):
            for c, cs in enumerate(chunks):
                nc.scalar.copy(out=planes[c][:, t, :], in_=pages[t][:, cs])
        copies = [nc.vector.tensor_copy if c % 2 == 0 else nc.scalar.copy for c in range(len(WIDTHS))]
        for c, cs in enumerate(chunks):
            copies[c](out=planes[c][:, PACK - 1, :], in_=pages[PACK - 1][:, cs])
        rounded = [held(f"rounded{c}", [P, w, PACK], BF16) for c, w in enumerate(WIDTHS)]
        for c in range(len(WIDTHS)):
            copies[c](
                out=rounded[c][:].rearrange("p (c i) t -> p c t i", i=4),
                in_=planes[c].rearrange("p t (c i) -> p c t i", i=4),
            )

        out_sc = held("out_sc", [P, T], U8)
        out_words = out_1[0].rearrange("p c i -> p (c i)").bitcast(I32)
        for c in range(len(WIDTHS)):
            cs = chunks[c]
            codes = held(f"codes{c}", [P, WIDTHS[c]], U32)
            nc.vector.quantize_mx(
                out=codes[:].bitcast(FP8X4), scales=out_sc[:, cs], in_=rounded[c][:].rearrange("p c t -> p (c t)")
            )
            nc.sync.dma_start(out=out_words[:, cs], in_=codes[:].bitcast(I32))
        for q in range(4):
            nc.scalar.dma_start(
                out=out_2[0, 4 * q : 4 * q + 4, :].bitcast(I32),
                in_=out_sc[QUADRANT * q : QUADRANT * q + 4, :].bitcast(I32),
            )
